import numpy as np, ml_dtypes
CORES = [66,74,82,90,194,202,210,218]
N = 8
import mx_ref
BF = ml_dtypes.bfloat16
def entries(a):
    return np.ascontiguousarray(a.T).reshape(-1)
def table(e):
    return np.ascontiguousarray(np.reshape(e, (-1, 16)).T).astype(np.int32)
def f(rng, *shape):
    return mx_ref.flush((rng.standard_normal(shape, dtype=np.float32) * np.exp2(rng.integers(-2, 3, shape[:-1] + (1,)))).astype(BF))
def wide(rng, *shape, cols=0):
    v = rng.standard_normal(shape, dtype=np.float32) * np.exp2(rng.integers(-12, 13, shape)).astype(np.float32)
    if cols: v *= np.repeat(np.exp2(rng.integers(-cols, cols + 1, shape[:-2] + (1, shape[-1] // 4))) * (rng.random(shape[:-2] + (1, shape[-1] // 4)) > 0.0625), 4, axis=-1).astype(np.float32)
    return mx_ref.flush(v.astype(BF))
T = 512
def listed(a):
    k = np.full((2 * N, 128), -1)
    for s in range(2 * N):
        i = np.flatnonzero(a == s); k[s, :len(i)] = i
    return k.reshape(-1)
def lists(rng, one=False, absent=False, sort=False, alike=False):
    t, a, k = [], [], []; nobody = rng.integers(0, N)
    for r in range(N):
        if r == 0 or not alike:
            u = np.concatenate([rng.permutation(8)[:2] for q in range(N)])
            if absent:
                here = rng.permutation([q for q in range(N) if q != nobody])[:T // 256 + r % 3].tolist()
                u.reshape(N, 2)[[q for q in range(N) if q not in here]] = -1
            else: u[rng.permutation(2 * N)[:rng.integers(0, 5)]] = -1
        v = rng.permutation(np.flatnonzero(u >= 0))
        if one: e = np.concatenate([np.full(128, v[0]), np.resize(v[1:], T - 128)])
        else:
            room = np.zeros(2 * N, int); room[v] = rng.integers(0, 129, len(v))
            for s in v:
                if room.sum() < T: room[s] = 128
            e = np.repeat(np.arange(2 * N), room)
        e = rng.permutation(e)[:T]
        if sort: e = np.sort(e)
        t.append(table(u)); a.append(table(e)); k.append(table(listed(e)))
    return {"tab": np.stack(t), "ad": np.stack(a), "tok": np.stack(k)}
def setup_inputs(rng):
    return {"x": f(rng, N, 128, 4 * T), "wa": f(rng, N, 1024, 512), **lists(rng)}
def setup_inputs_absent(rng):
    return {**setup_inputs(rng), **lists(rng, absent=True)}
def setup_inputs_alike(rng):
    return {**setup_inputs(rng), **lists(rng, alike=True)}
def setup_inputs_one(rng):
    return {**setup_inputs(rng), **lists(rng, one=True)}
def setup_inputs_sorted(rng):
    return {**setup_inputs(rng), **lists(rng, sort=True)}
def setup_inputs_spread(rng):
    d = setup_inputs(rng); d["x"] = wide(rng, N, 128, 4 * T, cols=8); return d
def check_inputs(d):
    b = []
    for n in ("x", "wa"):
        v = np.abs(np.asarray(d[n]).astype(np.float32))
        if not ((v == 0) | ((v >= 2.0 ** -30) & (v <= 2.0 ** 30))).all(): b.append(n)
    for r in range(N):
        u, a, k = entries(d["tab"][r]), entries(d["ad"][r]), entries(d["tok"][r]); p = u.reshape(N, 2)
        if u.min() < -1 or u.max() > 7 or ((p[:, 0] == p[:, 1]) & (p[:, 0] >= 0)).any(): b.append("tab")
        if a.min() < 0 or a.max() >= 2 * N or (u[a] < 0).any() or np.bincount(a).max() > 128: b.append("ad")
        elif (k != listed(a)).any(): b.append("tok")
    return b
def reference(x, wa, tab, ad, tok):
    y = np.zeros((N, 128, T), np.float32)
    for r in range(N):
        u, a, X = entries(tab[r]), entries(ad[r]), mx_ref.quantize(x[r])
        for s in range(2 * N):
            i = np.flatnonzero(a == s)
            if len(i) == 0: continue
            A = wa[s // 2][128 * u[s]:128 * u[s] + 128]
            y[r][:, i] = mx_ref.matmul(mx_ref.quantize(A), X)[:, i]
    return {"y": y}

@@ -1,0 +1,435 @@
+from concourse.bass import DstId, RemoteDMATransfer, IndirectOffsetOnAxis
+from concourse.mybir import dt, AluOpType, ActivationFunctionType
+
+NR = 8
+A = AluOpType
+COPY = ActivationFunctionType.Copy
+F8 = "float8_e4m3fn_x4"
+FB = 2048
+
+SCRATCH = {
+    "xt": ("sbuf", [128, 2048], "bfloat16"),
+    "wt": ("sbuf", [128, 4096], "bfloat16"),
+    "lt": ("dram", [NR, 128, 1], "int32"),
+    "tr": ("sbuf", [128, 16], "int32"),
+    "ot": ("sbuf", [128, 16], "int32"),
+    "lr": ("sbuf", [128, 16], "int32"),
+    "lb": ("sbuf", [128, 16], "int32"),
+    "mf": ("sbuf", [128, 16], "float32"),
+    "oa": ("sbuf", [128, 2], "int32"),
+    "oi": ("sbuf", [128, 2], "int32"),
+    "tk": ("sbuf", [128, 128], "int32"),
+    "xo": ("sbuf", [128, 128], "uint16"),
+    "ao": ("sbuf", [128, 448], "uint16"),
+    "pi": ("sbuf", [128, 1], "int32"),
+    "p112": ("sbuf", [128, 1], "int32"),
+    "pf": ("sbuf", [128, 1], "float32"),
+    "kf": ("sbuf", [128, 1], "float32"),
+    "bi": ("sbuf", [128, 32], "int32"),
+    "bo": ("sbuf", [128, 32], "int32"),
+    "j33": ("sbuf", [128, 16], "int32"),
+    "cf": ("sbuf", [128, 768], "float32"),
+    "vl": ("sbuf", [128, 256], "float32"),
+    "tg": ("sbuf", [128, 16], "int32"),
+    "pb": ("sbuf", [128, 16], "int32"),
+    "pc": ("sbuf", [128, 16], "int32"),
+    "pd": ("sbuf", [128, 16], "int32"),
+    "pe": ("sbuf", [128, 16], "int32"),
+    "pn": ("sbuf", [128, 16], "int32"),
+    "pj": ("sbuf", [128, 16], "int32"),
+    "ps": ("sbuf", [128, 16], "int32"),
+    "wo": ("sbuf", [128, 16], "uint16"),
+    "w8": ("sbuf", [128, 768], "float32"),
+    "dd": ("dram", [16, 8, 32], "float32"),
+    "e8": ("sbuf", [128, 256], "float32"),
+    "e4": ("sbuf", [128, 128], "float32"),
+    "e2": ("sbuf", [128, 64], "float32"),
+    "e1": ("sbuf", [128, 32], "float32"),
+    "em": ("sbuf", [128, 32], "float32"),
+    "ei": ("sbuf", [128, 32], "float32"),
+    "es": ("sbuf", [128, 32], "float32"),
+    "po": ("sbuf", [128, 32], "uint16"),
+    "ga": ("sbuf", [128, 7 * 1024], "bfloat16"),
+    "go": ("sbuf", [128, 1024], "bfloat16"),
+    "qc": ("sbuf", [128, 7 * 256], F8),
+    "qp": ("sbuf", [128, 7 * 256], "uint8"),
+    "ic": ("sbuf", [128, 2048], F8),
+    "ip": ("sbuf", [128, 2048], "uint8"),
+    "hc": ("sbuf", [128, 768], F8),
+    "hp": ("sbuf", [128, 768], "uint8"),
+    "hx": ("sbuf", [128, 8192], "bfloat16"),
+    "xc": ("sbuf", [128, 2048], F8),
+    "xp": ("sbuf", [128, 2048], "uint8"),
+    "fc": ("sbuf", [128, 512], F8),
+    "fp": ("sbuf", [128, 512], "uint8"),
+    "pm": ("psum", [128, 4096], "float32"),
+    "res": ("sbuf", [128, FB + 3072], "float32"),
+    "yt": ("sbuf", [128, 512], "float32"),
+}
+
+SEMAPHORES = (["s_lt", "s_tr", "s_x", "s_wa", "s_tk", "s_tg", "s_dd", "s_e8", "s_li", "s_lr", "s_y0", "s_y1", "s_own", "s_k",
+               "s_pb1", "s_pb2", "s_oi", "s_sent", "s_ls", "s_go", "vv", "s_xo", "s_w8", "s_po", "s_oq", "s_yv", "s_ys", "s_cf",
+               "s_vl", "s_kv", "s_fq", "s_ho", "h_c0", "h_p0", "h_c1", "h_p1", "h_c3", "h_p3"]
+              + ["ar%d" % i for i in range(NR)] + ["mm%d" % i for i in range(NR)] + ["ev%d" % i for i in range(NR)]
+              + ["ao%d" % i for i in range(7)] + ["sa%d" % i for i in range(7)] + ["va%d" % i for i in range(7)]
+              + ["vq%d" % i for i in range(7)]
+              + ["sx%d" % i for i in range(3)] + ["vx%d" % i for i in range(3)] + ["xq%d" % i for i in range(3)])
+
+SPLIT = 640
+S_PRE = [(0, 0), (0, 1), (0, 2), (1, 0), (1, 1)]
+V_PRE = [(0, 3), (1, 2)]
+S_POST = [(1, 3), (2, 0), (2, 1), (2, 2), (2, 3)]
+V_POST = []
+HOPS = {0: 0, 1: 1, 3: 2}
+CALLS = [[(0, 0, None)], [(0, 1, None)], [(1, 0, None), (2, 0, None)], [(1, 1, None), (2, 1, None)],
+         [(3, 0, None), (4, 0, None)], [(3, 1, None), (4, 1, None)], [(5, 0, None)], [(6, 0, None)], [(5, 1, 0), (6, 1, 1)]]
+
+
+def mask_of(engines):
+    return sum(1 << e for e in engines)
+
+
+def roads(me, cores, topo):
+    c = cores[me]
+    others = sorted([r for r in range(NR) if r != me], key=lambda r: r ^ me)
+    mate = [r for r in others if topo.mates(c, cores[r])]
+    same = [r for r in others if topo.same_plane(c, cores[r])]
+    cross = [r for r in others if r not in mate and r not in same]
+    far = [h for h in topo.cores_of(c) if topo.die(h) != topo.die(c) and all(topo.may_write(h, cores[r]) for r in others)]
+    order = [cross[1], cross[2], cross[0], same[2], mate[0], same[0], same[1]]
+    return order, far[0]
+
+
+def dst(topo, d, src):
+    rid, pid = topo.addr(d, src)
+    return DstId(rid=rid, pnc=pid)
+
+
+def codes(v):
+    return v.bitcast(dt.uint8)
+
+
+def on_chip(topo, src, hand, away):
+    out = topo.engines(src, away)
+    return [e for e in topo.engines(src, hand) if e not in out]
+
+
+def helper_program(g, core, T, topo, me):
+    cores = list(T.cores)
+    order, far = roads(me, cores, topo)
+    if core != far:
+        return
+    sent = 0
+    for pos in sorted(HOPS):
+        r = order[pos]
+        at = 256 * HOPS[pos]
+        n = len(on_chip(topo, cores[me], core, cores[r]))
+        eng = topo.engines(core, cores[r])
+        for what in (0, 1):
+            g.wait_ge(T.sem["h_%s%d" % ("cp"[what], pos)], n)
+            if what == 0:
+                s, d = codes(T.hc[:, at:at + 256]), codes(T.ic[:, 256 * me:256 * me + 256])
+            else:
+                s, d = T.hp[:, at:at + 256], T.ip[:, 256 * me:256 * me + 256]
+            g.remote_dma_fused([RemoteDMATransfer(dst_ids=[dst(topo, cores[r], core)], dma_engine_mask=mask_of(eng),
+                                                  remote_sem=T.sem["ar%d" % me], src=s, dst=d)], local_sem=T.sem.s_sent)
+            sent += len(eng)
+    g.wait_ge(T.sem.s_sent, sent)
+
+
+def arrivals(r, me, cores, topo):
+    order, far = roads(r, cores, topo)
+    pos = order.index(me)
+    n = len(topo.engines(far if pos in HOPS else cores[r], cores[me]))
+    return sum(n if half is None else n // 2 for call in CALLS for i, what, half in call if i == pos)
+
+
+def rank_program(g, core, T, topo):
+    rank = T.rank_of(core)
+    cores = list(T.cores)
+    if rank is None:
+        for r in range(NR):
+            if core in topo.cores_of(cores[r]):
+                helper_program(g, core, T, topo, r)
+        return
+    me = rank
+    order, far = roads(me, cores, topo)
+    S = T.sem
+    v, s, pe, sy = g.vector, g.scalar, g.tensor, g.sync
+    full = [me, order[4], order[2]]
+    two = [k for k in range(4) if 2 * k not in full and 2 * k + 1 not in full]
+    rest = [r for r in range(NR) if r not in full and r // 2 not in two]
+    runs = [(2 * two[0], 2), (2 * two[1], 2), (rest[0], 1)]
+
+    def run_of(r):
+        return [k for k in range(3) if runs[k][0] <= r < runs[k][0] + runs[k][1]][0]
+
+    def wa_load(a, b):
+        for m in range(a, b):
+            sy.dma_start(T.wt[:, 512 * m:512 * m + 512], T.wa[128 * m:128 * m + 128, :]).then_inc(S.s_wa, 16)
+
+    sy.dma_start(T.lt[me, 0:16, 0], T.tab[:, 0]).then_inc(S.s_lt, 16)
+    sy.dma_start(T.lt[me, 16:128, 0], T.tok[0, 0:112]).then_inc(S.s_lt, 16)
+    sy.dma_start(T.tr[0:1, 0:16], T.tab[:, 0]).then_inc(S.s_tr, 16)
+    for q in range(4):
+        sy.dma_start(T.tk[16 * q:16 * q + 16, :], T.tok[:]).then_inc(S.s_tk, 16)
+    sy.dma_start(T.xt[:], T.x[:]).then_inc(S.s_x, 16)
+    wa_load(0, 3)
+    sy.wait_ge(S.s_kv, 1)
+    sy.wait_ge(S.s_cf, 6)
+    for f, q in enumerate(full):
+        sy.dma_start(T.vl[16 * q:16 * q + 1, :], T.cf[0:1, 256 * f:256 * f + 256]).then_inc(S.s_vl, 16)
+    sy.wait_ge(S.s_go, 1)
+    wa_load(3, 6)
+    sy.wait_ge(S.s_li, 7)
+    sy.wait_ge(S.s_lt, 32)
+    sy.dma_start(T.lr[0:1, 0:16], T.lt[:, 2 * me:2 * me + 2, 0]).then_inc(S.s_lr, 16)
+    wa_load(6, 8)
+    sy.wait_ge(S.s_w8, 1)
+    for q in range(8):
+        sy.dma_start(T.dd[:, q, :], T.w8[16 * q:16 * q + 1, 0:512]).then_inc(S.s_dd, 16)
+    sy.wait_ge(S.s_dd, 128)
+    for q in range(8):
+        sy.dma_start(T.e8[16 * q:16 * q + 16, 0:256], T.dd[:]).then_inc(S.s_e8, 16)
+    sy.wait_ge(S.s_yv, 1)
+    sy.dma_start(T.y[:, 0:256], T.yt[:, 0:256]).then_inc(S.s_y0, 16)
+    sy.wait_ge(S.s_y0, 16)
+
+    def own_adapter(k):
+        g.indirect_dma_start(T.go[:, 512 * k:512 * k + 512], None, T.wa[:],
+                             IndirectOffsetOnAxis(ap=T.oi[:, k:k + 1], axis=0), bounds_check=1023).then_inc(S.s_own, 16)
+
+    g.iota(T.pi[:], [[1, 1]], 0, 1).then_inc(S.s_k, 1)
+    g.iota(T.bi[:], [[16, 32]], 0, 1).then_inc(S.s_k, 1)
+    g.iota(T.vl[:], [[1, 256]], 0, 16, allow_small_or_imprecise_dtypes=True).then_inc(S.s_kv, 1)
+    g.wait_ge(S.s_tr, 16)
+    g.partition_broadcast(T.ot[:], T.tr[0:1, 0:16], 128).then_inc(S.s_pb1, 1)
+    g.wait_ge(S.s_lt, 32)
+    one = topo.engines(core, cores[order[0]])[:1]
+    g.remote_dma_fused([RemoteDMATransfer(dst_ids=[dst(topo, cores[r], core) for r in order], dma_engine_mask=mask_of(one),
+                                          remote_sem=S.s_li, srcs=[T.lt[me]], dsts=[T.lt[me] for r in order])],
+                       local_sem=S.s_ls)
+    g.sem_inc(S.s_go, 1)
+    g.wait_ge(S.s_oi, 1)
+    own_adapter(0)
+    g.wait_ge(S.s_lr, 16)
+    g.partition_broadcast(T.lb[:], T.lr[0:1, 0:16], 128).then_inc(S.s_pb2, 1)
+    own_adapter(1)
+
+    def move(pos, what, half):
+        a = (codes(T.qc[:, 256 * pos:256 * pos + 256]), T.qp[:, 256 * pos:256 * pos + 256])[what]
+        if pos in HOPS:
+            to = far
+            eng = on_chip(topo, core, to, cores[order[0]])
+            at = 256 * HOPS[pos]
+            b = (codes(T.hc[:, at:at + 256]), T.hp[:, at:at + 256])[what]
+            sem = S["h_%s%d" % ("cp"[what], pos)]
+        else:
+            to = cores[order[pos]]
+            eng = topo.engines(core, to)
+            b = (codes(T.ic[:, 256 * me:256 * me + 256]), T.ip[:, 256 * me:256 * me + 256])[what]
+            sem = S["ar%d" % me]
+        if half is not None:
+            w = len(eng) // 2
+            eng = eng[half * w:half * w + w]
+        return RemoteDMATransfer(dst_ids=[dst(topo, to, core)], dma_engine_mask=mask_of(eng), remote_sem=sem, src=a, dst=b), len(eng)
+
+    sent = 0
+    for call in CALLS:
+        ts = []
+        for i, what, half in call:
+            g.wait_ge(S["vq%d" % i], 1)
+            t, n = move(i, what, half)
+            ts.append(t)
+            sent += n
+        g.remote_dma_fused(ts, local_sem=S.s_sent)
+    g.wait_ge(S.s_ls, 1)
+    g.wait_ge(S.s_sent, sent)
+
+    for q in range(4, 8):
+        s.dma_start(T.tk[16 * q:16 * q + 16, :], T.tok[:]).then_inc(S.s_tk, 16)
+    for q in range(8):
+        s.dma_start(T.tg[16 * q:16 * q + 16, :], T.tok[:, 16 * q:16 * q + 16]).then_inc(S.s_tg, 16)
+
+    def xgather(k, t):
+        r, n = runs[k]
+        return (T.hx[:, 1024 * r + t:1024 * (r + n):4], T.xt[:, t:2048].indirect(T.xo[:, 16 * r:16 * (r + n)]))
+
+    s.wait_ge(S.s_xo, 1)
+    s.wait_ge(S.s_x, 16)
+    for k, t in S_PRE:
+        o, i = xgather(k, t)
+        s.activation(o, i, COPY).then_inc(S["sx%d" % k], 1)
+    s.wait_ge(S.s_wa, 128)
+    for i in range(7):
+        s.wait_ge(S["ao%d" % i], 2)
+        s.activation(T.ga[:, 1024 * i:1024 * i + SPLIT],
+                     T.wt[:].indirect(T.ao[:, 64 * i:64 * i + SPLIT // 16]), COPY).then_inc(S["sa%d" % i], 1)
+    for k, t in S_POST:
+        o, i = xgather(k, t)
+        s.activation(o, i, COPY).then_inc(S["sx%d" % k], 1)
+
+    src = [me, order[2], order[4], order[0], order[1], order[5], order[3], order[6]]
+
+    def evac(k, n):
+        b = 2 * (n % 4) + k
+        if src[n] in full:
+            at, w = FB + 1024 * full.index(src[n]) + 512 * k, 512
+        else:
+            at, w = 128 * (2 * src[n] + k), 128
+        return T.res[:, at:at + w], T.pm[:, 512 * b:512 * b + w]
+
+    for n in range(NR):
+        s.wait_ge(S["mm%d" % n], 2)
+        o, i = evac(1, n)
+        s.activation(o, i, COPY).then_inc(S["ev%d" % n], 1)
+    s.wait_ge(S.s_po, 1)
+    s.wait_ge(S.s_ho, 3)
+    for n in range(NR):
+        s.wait_ge(S["ev%d" % n], 2)
+    s.activation(T.yt[:, 256:512], T.res[:].indirect(T.po[:, 16:32]), COPY).then_inc(S.s_ys, 1)
+    s.wait_ge(S.s_ys, 1)
+    s.dma_start(T.y[:, 256:512], T.yt[:, 256:512]).then_inc(S.s_y1, 16)
+    s.wait_ge(S.s_y1, 16)
+
+    for n in range(NR):
+        r = src[n]
+        if r in full:
+            pe.wait_ge(S.s_fq, 1)
+        else:
+            pe.wait_ge(S["xq%d" % run_of(r)], 1)
+        if r == me:
+            pe.wait_ge(S.s_oq, 1)
+        else:
+            pe.wait_ge(S["ar%d" % r], arrivals(r, me, cores, topo))
+        if n >= 4:
+            pe.wait_ge(S["ev%d" % (n - 4)], 2)
+        for k in range(2):
+            c = 128 * (2 * r + k)
+            b = 2 * (n % 4) + k
+            if r in full:
+                o, xc, xp = T.pm[:, 512 * b:512 * b + 512], T.fc[:, 0:512], T.fp[:, 0:512]
+            else:
+                o, xc, xp = T.pm[:, 512 * b:512 * b + 128], T.xc[:, c:c + 128], T.xp[:, c:c + 128]
+            pe.matmul_mx(o, T.ic[:, c:c + 128], T.ip[:, c:c + 128], xc, xp, True, True).then_inc(S["mm%d" % n], 1)
+
+    cnt = [0]
+
+    def dep(inst):
+        inst.then_inc(S.vv, 1)
+        cnt[0] += 1
+
+    def done():
+        v.wait_ge(S.vv, cnt[0])
+
+    dep(v.memset(T.w8[:, 0:512], 0.0))
+    for f in range(6):
+        v.memset(T.cf[:, 128 * f:128 * f + 128], float(FB + 512 * f)).then_inc(S.s_cf, 1)
+    v.wait_ge(S.s_k, 2)
+    dep(v.tensor_scalar(T.p112[:], T.pi[:], 112, None, A.bitwise_and))
+    dep(v.tensor_copy(T.pf[:], T.pi[:]))
+    done()
+    dep(v.tensor_copy(T.kf[:], T.p112[:]))
+    done()
+    dep(v.tensor_scalar(T.bo[:], T.bi[:], T.kf[:], None, A.subtract))
+    done()
+    dep(v.tensor_scalar(T.j33[:], T.bo[:, 0:16], 33.0, None, A.add))
+    v.wait_ge(S.s_tk, 128)
+    v.tensor_scalar(T.xo[:], T.tk[:], 0.0, 4.0, A.max, A.mult).then_inc(S.s_xo, 1)
+    v.wait_ge(S.s_pb1, 1)
+    dep(v.tensor_scalar(T.oa[:], T.ot[:, 2 * me:2 * me + 2], 0.0, 128.0, A.max, A.mult))
+    done()
+    v.tensor_scalar(T.oi[:], T.oa[:], T.pf[:], None, A.add).then_inc(S.s_oi, 1)
+    for r in full:
+        v.memset(T.res[:, 256 * r:256 * r + 256], 0.0).then_inc(S.s_ho, 1)
+
+    v.wait_ge(S.s_xo, 1)
+    v.wait_ge(S.s_x, 16)
+
+    def vx(lst):
+        for k, t in lst:
+            o, i = xgather(k, t)
+            v.tensor_copy(o, i).then_inc(S["vx%d" % k], 1)
+
+    def xquant(k):
+        nv, ns = sum(1 for a in V_PRE + V_POST if a[0] == k), sum(1 for a in S_PRE + S_POST if a[0] == k)
+        if nv:
+            v.wait_ge(S["vx%d" % k], nv)
+        if ns:
+            v.wait_ge(S["sx%d" % k], ns)
+        r, n = runs[k]
+        v.quantize_mx(T.xc[:, 256 * r:256 * (r + n)], T.xp[:, 256 * r:256 * (r + n)],
+                      T.hx[:, 1024 * r:1024 * (r + n)]).then_inc(S["xq%d" % k], 1)
+
+    vx(V_PRE)
+    v.quantize_mx(T.fc[:, 0:512], T.fp[:, 0:512], T.xt[:, 0:2048]).then_inc(S.s_fq, 1)
+    v.wait_ge(S.s_tg, 128)
+    dep(v.tensor_scalar(T.pb[:], T.tg[:], 4, None, A.arith_shift_right))
+    dep(v.tensor_scalar(T.pc[:], T.tg[:], 32.0, None, A.mult))
+    dep(v.tensor_scalar(T.pn[:], T.tg[:], 0.0, None, A.is_lt))
+    done()
+    dep(v.tensor_scalar(T.pd[:], T.pb[:], -511.0, None, A.mult))
+    dep(v.tensor_tensor(T.pj[:], T.pn[:], T.j33[:], A.mult))
+    done()
+    dep(v.tensor_tensor(T.pe[:], T.pc[:], T.pd[:], A.add))
+    done()
+    dep(v.tensor_tensor(T.ps[:], T.pe[:], T.pj[:], A.add))
+    done()
+    dep(v.tensor_copy(T.wo[:], T.ps[:]))
+    done()
+    v.wait_ge(S.s_kv, 1)
+    v.wait_ge(S.s_vl, 48)
+    v.tensor_copy(T.w8[:].indirect(T.wo[:]), T.vl[:]).then_inc(S.s_w8, 1)
+    xquant(0)
+
+    v.wait_ge(S.s_pb2, 1)
+    dep(v.tensor_scalar(T.mf[:], T.lb[:], 0.0, 512.0, A.max, A.mult))
+    done()
+
+    def offsets(i):
+        for k in range(2):
+            a = 2 * order[i] + k
+            c = 64 * i + 32 * k
+            v.tensor_scalar(T.ao[:, c:c + 32], T.bo[:], T.mf[:, a:a + 1], None, A.add).then_inc(S["ao%d" % i], 1)
+
+    offsets(0)
+    v.wait_ge(S.s_wa, 128)
+    for i in range(7):
+        if i < 6:
+            offsets(i + 1)
+        v.wait_ge(S["ao%d" % i], 2)
+        v.tensor_copy(T.ga[:, 1024 * i + SPLIT:1024 * i + 1024],
+                      T.wt[:].indirect(T.ao[:, 64 * i + SPLIT // 16:64 * i + 64])).then_inc(S["va%d" % i], 1)
+        v.wait_ge(S["va%d" % i], 1)
+        v.wait_ge(S["sa%d" % i], 1)
+        v.quantize_mx(T.qc[:, 256 * i:256 * i + 256], T.qp[:, 256 * i:256 * i + 256],
+                      T.ga[:, 1024 * i:1024 * i + 1024]).then_inc(S["vq%d" % i], 1)
+        if i == 3:
+            v.wait_ge(S.s_own, 32)
+            v.quantize_mx(T.ic[:, 256 * me:256 * me + 256], T.ip[:, 256 * me:256 * me + 256], T.go[:]).then_inc(S.s_oq, 1)
+    vx(V_POST)
+    v.wait_ge(S.s_e8, 128)
+    dep(v.tensor_tensor(T.e4[:], T.e8[:, 0:128], T.e8[:, 128:256], A.add))
+    done()
+    dep(v.tensor_tensor(T.e2[:], T.e4[:, 0:64], T.e4[:, 64:128], A.add))
+    done()
+    dep(v.tensor_tensor(T.e1[:], T.e2[:, 0:32], T.e2[:, 32:64], A.add))
+    done()
+    dep(v.tensor_scalar(T.em[:], T.e1[:], float(FB), None, A.is_ge))
+    done()
+    dep(v.tensor_tensor(T.ei[:], T.em[:], T.bo[:], A.mult))
+    done()
+    dep(v.tensor_tensor(T.es[:], T.e1[:], T.ei[:], A.add))
+    done()
+    v.tensor_copy(T.po[:], T.es[:]).then_inc(S.s_po, 1)
+    xquant(1)
+    xquant(2)
+    for n in range(NR):
+        v.wait_ge(S["mm%d" % n], 2)
+        o, i = evac(0, n)
+        v.tensor_copy(o, i).then_inc(S["ev%d" % n], 1)
+    v.wait_ge(S.s_po, 1)
+    v.wait_ge(S.s_ho, 3)
+    for n in range(NR):
+        v.wait_ge(S["ev%d" % n], 2)
+    v.tensor_copy(T.yt[:, 0:256], T.res[:].indirect(T.po[:, 0:16])).then_inc(S.s_yv, 1)

@@ -5,38 +5,39 @@ NR = 8
 A = AluOpType
 COPY = ActivationFunctionType.Copy
 F8 = "float8_e4m3fn_x4"
-FB = 2048
+GB = 3072
 
 SCRATCH = {
     "xt": ("sbuf", [128, 2048], "bfloat16"),
     "wt": ("sbuf", [128, 4096], "bfloat16"),
     "lt": ("dram", [NR, 128, 1], "int32"),
-    "tr": ("sbuf", [128, 16], "int32"),
-    "ot": ("sbuf", [128, 16], "int32"),
-    "lr": ("sbuf", [128, 16], "int32"),
-    "lb": ("sbuf", [128, 16], "int32"),
-    "mf": ("sbuf", [128, 16], "float32"),
-    "oa": ("sbuf", [128, 2], "int32"),
+    "tr": ("sbuf", [128, 4], "int32"),
+    "lr": ("sbuf", [128, 4], "int32"),
+    "zo": ("sbuf", [128, 32], "float32"),
+    "mo": ("sbuf", [128, 32], "float32"),
+    "zl": ("sbuf", [128, 32], "float32"),
+    "mf": ("sbuf", [128, 32], "float32"),
     "oi": ("sbuf", [128, 2], "int32"),
+    "ri": ("sbuf", [128, 16], "int32"),
     "tk": ("sbuf", [128, 128], "int32"),
     "xo": ("sbuf", [128, 128], "uint16"),
     "ao": ("sbuf", [128, 448], "uint16"),
+    "z0": ("sbuf", [128, 2], "uint16"),
     "pi": ("sbuf", [128, 1], "int32"),
     "p112": ("sbuf", [128, 1], "int32"),
     "pf": ("sbuf", [128, 1], "float32"),
     "kf": ("sbuf", [128, 1], "float32"),
+    "c0": ("sbuf", [128, 1], "float32"),
+    "c1": ("sbuf", [128, 1], "float32"),
     "bi": ("sbuf", [128, 32], "int32"),
     "bo": ("sbuf", [128, 32], "int32"),
-    "j33": ("sbuf", [128, 16], "int32"),
-    "cf": ("sbuf", [128, 768], "float32"),
+    "jk": ("sbuf", [128, 16], "int32"),
     "vl": ("sbuf", [128, 256], "float32"),
     "tg": ("sbuf", [128, 16], "int32"),
+    "pa": ("sbuf", [128, 16], "int32"),
     "pb": ("sbuf", [128, 16], "int32"),
     "pc": ("sbuf", [128, 16], "int32"),
     "pd": ("sbuf", [128, 16], "int32"),
-    "pe": ("sbuf", [128, 16], "int32"),
-    "pn": ("sbuf", [128, 16], "int32"),
-    "pj": ("sbuf", [128, 16], "int32"),
     "ps": ("sbuf", [128, 16], "int32"),
     "wo": ("sbuf", [128, 16], "uint16"),
     "w8": ("sbuf", [128, 768], "float32"),
@@ -55,34 +56,58 @@ SCRATCH = {
     "qp": ("sbuf", [128, 7 * 256], "uint8"),
     "ic": ("sbuf", [128, 2048], F8),
     "ip": ("sbuf", [128, 2048], "uint8"),
-    "hc": ("sbuf", [128, 768], F8),
-    "hp": ("sbuf", [128, 768], "uint8"),
-    "hx": ("sbuf", [128, 8192], "bfloat16"),
-    "xc": ("sbuf", [128, 2048], F8),
-    "xp": ("sbuf", [128, 2048], "uint8"),
+    "hc": ("sbuf", [128, 1280], F8),
+    "hp": ("sbuf", [128, 1280], "uint8"),
+    "hx": ("sbuf", [128, 5120], "bfloat16"),
+    "xc": ("sbuf", [128, 1280], F8),
+    "xp": ("sbuf", [128, 1280], "uint8"),
     "fc": ("sbuf", [128, 512], F8),
     "fp": ("sbuf", [128, 512], "uint8"),
     "pm": ("psum", [128, 4096], "float32"),
-    "res": ("sbuf", [128, FB + 3072], "float32"),
+    "res": ("sbuf", [128, GB + 1280], "float32"),
     "yt": ("sbuf", [128, 512], "float32"),
 }
 
 SEMAPHORES = (["s_lt", "s_tr", "s_x", "s_wa", "s_tk", "s_tg", "s_dd", "s_e8", "s_li", "s_lr", "s_y0", "s_y1", "s_own", "s_k",
-               "s_pb1", "s_pb2", "s_oi", "s_sent", "s_ls", "s_go", "vv", "s_xo", "s_w8", "s_po", "s_oq", "s_yv", "s_ys", "s_cf",
-               "s_vl", "s_kv", "s_fq", "s_ho", "h_c0", "h_p0", "h_c1", "h_p1", "h_c3", "h_p3"]
-              + ["ar%d" % i for i in range(NR)] + ["mm%d" % i for i in range(NR)] + ["ev%d" % i for i in range(NR)]
-              + ["ao%d" % i for i in range(7)] + ["sa%d" % i for i in range(7)] + ["va%d" % i for i in range(7)]
-              + ["vq%d" % i for i in range(7)]
-              + ["sx%d" % i for i in range(3)] + ["vx%d" % i for i in range(3)] + ["xq%d" % i for i in range(3)])
+               "s_z", "s_oi", "s_ri", "s_sent", "s_ls", "s_go", "vv", "s_xo", "s_w8", "s_po", "s_oq", "s_yv", "s_ys",
+               "s_kv", "s_fq"] + ["h%d" % i for i in range(12)]
+              + ["ar%d" % i for i in range(NR)] + ["mm%d" % i for i in range(2 * NR)] + ["ev%d" % i for i in range(2 * NR)]
+              + ["ao%d" % i for i in range(7)] + ["ga%d" % i for i in range(7)]
+              + ["vq%d" % i for i in range(7)] + ["gi%d" % i for i in range(7)]
+              + ["vp%d" % i for i in range(7)] + ["gp%d" % i for i in range(7)]
+              + ["gx%d" % i for i in range(3)] + ["xq%d" % i for i in range(3)])
 
-SPLIT = 640
-S_PRE = [(0, 0), (0, 1), (0, 2), (1, 0), (1, 1)]
-V_PRE = [(0, 3), (1, 2)]
-S_POST = [(1, 3), (2, 0), (2, 1), (2, 2), (2, 3)]
-V_POST = []
-HOPS = {0: 0, 1: 1, 3: 2}
-CALLS = [[(0, 0, None)], [(0, 1, None)], [(1, 0, None), (2, 0, None)], [(1, 1, None), (2, 1, None)],
-         [(3, 0, None), (4, 0, None)], [(3, 1, None), (4, 1, None)], [(5, 0, None)], [(6, 0, None)], [(5, 1, 0), (6, 1, 1)]]
+ORDER = [("x", 2), ("x", 0), ("s", 1), ("s", 2), ("x", 1), ("s", 0), ("m", 0)]
+HOPS = {0: 0, 1: 0, 3: 0}
+HALF = {0: 0}
+EARLY = [0]
+FULL = [2, 4]
+RUNS = [[0, 3], [1, 5], [6]]
+SRC = [-1, 2, 4, 0, 1, 5, 3, 6]
+WA_EARLY = 1
+WA_MID = 7
+
+
+def cod(*pos):
+    return [(i, 0, None, None) for i in pos]
+
+
+def pla(*pos):
+    return [(i, 1, None, None) for i in pos]
+
+
+G_PLAN = [("own", 0), ("own", 1), [(0, 0, 0, None)], [(0, 0, 1, None)], pla(0),
+          cod(1, 2), pla(1, 2), cod(3), cod(4), pla(3, 4), cod(5), pla(5), cod(6), pla(6)]
+SHARE = {1: 672, 2: 672, 3: 672, 4: 672, 5: 640, 6: 640}
+S_PLAN = ([("x", 0, 0), ("x", 0, 1), ("x", 0, 2), ("x", 1, 0), ("x", 1, 1), ("a", 0, 0, 224), ("a", 0, 512, 800)]
+          + [("a", i, 0, SHARE[i]) for i in range(1, 7)]
+          + [("x", 1, 2), ("x", 2, 0), ("x", 2, 1), ("x", 2, 2), ("x", 2, 3)] + [("e", n, 1) for n in range(8)])
+V_PLAN = ([("x", 0, 3), "o1", ("fq", 0), "o2", ("fq", 1), "o3", "o4", "o5", "scatter", ("xq", 0), "list"]
+          + [("of", 0), ("of", 1), ("a", 0, 224, 512), ("q0", 0), ("a", 0, 800, 1024), ("of", 2), ("q", 0)]
+          + [x for i in range(1, 5) for x in (("a", i, SHARE[i], 1024), ("of", i + 2), ("q", i))]
+          + [x for i in range(5, 7) for x in (("a", i, SHARE[i], 1024), ("q", i))]
+          + ["oq", ("x", 1, 3), "e4", ("xq", 1), "e2", ("e", 0, 0), "e1", ("e", 1, 0), "em", ("xq", 2), "ei", ("e", 2, 0), "es",
+             ("e", 3, 0), "po"] + [("e", n, 0) for n in range(4, 8)])
 
 
 def mask_of(engines):
@@ -94,10 +119,10 @@ def roads(me, cores, topo):
     others = sorted([r for r in range(NR) if r != me], key=lambda r: r ^ me)
     mate = [r for r in others if topo.mates(c, cores[r])]
     same = [r for r in others if topo.same_plane(c, cores[r])]
-    cross = [r for r in others if r not in mate and r not in same]
-    far = [h for h in topo.cores_of(c) if topo.die(h) != topo.die(c) and all(topo.may_write(h, cores[r]) for r in others)]
-    order = [cross[1], cross[2], cross[0], same[2], mate[0], same[0], same[1]]
-    return order, far[0]
+    cross = [[q for q in others if topo.mates(cores[r], cores[q])][0] for r in same]
+    free = [h for h in topo.cores_of(c) if h != c and all(topo.may_write(h, cores[r]) for r in others)]
+    hands = [h for h in free if topo.die(h) != topo.die(c)] + [h for h in free if topo.die(h) == topo.die(c)]
+    return [{"s": same, "x": cross, "m": mate}[kind][k] for kind, k in ORDER], hands
 
 
 def dst(topo, d, src):
@@ -109,39 +134,73 @@ def codes(v):
     return v.bitcast(dt.uint8)
 
 
-def on_chip(topo, src, hand, away):
-    out = topo.engines(src, away)
-    return [e for e in topo.engines(src, hand) if e not in out]
+def hops(piece):
+    return piece[0] in HOPS and HALF.get(piece[0], piece[2]) == piece[2]
+
+
+def first(step):
+    return step[1] in EARLY and step[3] <= 512
+
+
+def pieces():
+    return [x for call in G_PLAN if call[0] not in ("i", "own") for x in call]
+
+
+def sides(a, b, i, j, what, part):
+    lo, w = (0, 256) if part is None else (128 * part, 128)
+    s, d = a[what][:, 256 * i + lo:256 * i + lo + w], b[what][:, 256 * j + lo:256 * j + lo + w]
+    return (s, d) if what else (codes(s), codes(d))
+
+
+def engines_of(piece, src, to, away, topo):
+    eng = topo.engines(src, to)
+    if piece[3] == "out":
+        eng = topo.engines(src, away)
+    elif hops(piece) and piece[3] != "all":
+        eng = [e for e in eng if e not in topo.engines(src, away)]
+    if piece[3] in (0, 1):
+        w = len(eng) // 2
+        eng = eng[piece[3] * w:piece[3] * w + w]
+    return eng
+
+
+def onward(piece, hand, to, topo):
+    call = [c for c in G_PLAN if piece in c][0]
+    both = [x for x in call if hops(x) and HOPS[x[0]] == HOPS[piece[0]]]
+    eng = topo.engines(hand, to)
+    w = len(eng) // len(both)
+    return eng[w * both.index(piece):w * both.index(piece) + w]
 
 
 def helper_program(g, core, T, topo, me):
     cores = list(T.cores)
-    order, far = roads(me, cores, topo)
-    if core != far:
-        return
+    order, hands = roads(me, cores, topo)
     sent = 0
-    for pos in sorted(HOPS):
-        r = order[pos]
-        at = 256 * HOPS[pos]
-        n = len(on_chip(topo, cores[me], core, cores[r]))
-        eng = topo.engines(core, cores[r])
-        for what in (0, 1):
-            g.wait_ge(T.sem["h_%s%d" % ("cp"[what], pos)], n)
-            if what == 0:
-                s, d = codes(T.hc[:, at:at + 256]), codes(T.ic[:, 256 * me:256 * me + 256])
-            else:
-                s, d = T.hp[:, at:at + 256], T.ip[:, 256 * me:256 * me + 256]
-            g.remote_dma_fused([RemoteDMATransfer(dst_ids=[dst(topo, cores[r], core)], dma_engine_mask=mask_of(eng),
-                                                  remote_sem=T.sem["ar%d" % me], src=s, dst=d)], local_sem=T.sem.s_sent)
+    hopping = [x for x in pieces() if hops(x)]
+    for call in G_PLAN:
+        ts = []
+        for piece in call:
+            if piece not in hopping or hands[HOPS[piece[0]]] != core:
+                continue
+            pos, what, part = piece[:3]
+            r = order[pos]
+            eng = onward(piece, core, cores[r], topo)
+            g.wait_ge(T.sem["h%d" % hopping.index(piece)], len(engines_of(piece, cores[me], core, cores[r], topo)))
+            s, d = sides((T.hc, T.hp), (T.ic, T.ip), sorted(HOPS).index(pos), me, what, part)
+            ts.append(RemoteDMATransfer(dst_ids=[dst(topo, cores[r], core)], dma_engine_mask=mask_of(eng),
+                                        remote_sem=T.sem["ar%d" % me], src=s, dst=d))
             sent += len(eng)
-    g.wait_ge(T.sem.s_sent, sent)
+        if ts:
+            g.remote_dma_fused(ts, local_sem=T.sem.s_sent)
+    if sent:
+        g.wait_ge(T.sem.s_sent, sent)
 
 
 def arrivals(r, me, cores, topo):
-    order, far = roads(r, cores, topo)
+    order, hands = roads(r, cores, topo)
     pos = order.index(me)
-    n = len(topo.engines(far if pos in HOPS else cores[r], cores[me]))
-    return sum(n if half is None else n // 2 for call in CALLS for i, what, half in call if i == pos)
+    return sum(len(onward(x, hands[HOPS[pos]], cores[me], topo) if hops(x) else engines_of(x, cores[r], cores[me], cores[me], topo))
+               for x in pieces() if x[0] == pos)
 
 
 def rank_program(g, core, T, topo):
@@ -153,38 +212,36 @@ def rank_program(g, core, T, topo):
                 helper_program(g, core, T, topo, r)
         return
     me = rank
-    order, far = roads(me, cores, topo)
+    order, hands = roads(me, cores, topo)
     S = T.sem
     v, s, pe, sy = g.vector, g.scalar, g.tensor, g.sync
-    full = [me, order[4], order[2]]
-    two = [k for k in range(4) if 2 * k not in full and 2 * k + 1 not in full]
-    rest = [r for r in range(NR) if r not in full and r // 2 not in two]
-    runs = [(2 * two[0], 2), (2 * two[1], 2), (rest[0], 1)]
+    full = [me] + [order[i] for i in FULL]
+    runs = [sorted(order[i] for i in run) for run in RUNS]
+    gathered = [r for run in runs for r in run]
+    src = [me if i < 0 else order[i] for i in SRC]
 
     def run_of(r):
-        return [k for k in range(3) if runs[k][0] <= r < runs[k][0] + runs[k][1]][0]
+        return [k for k in range(3) if r in runs[k]][0]
 
     def wa_load(a, b):
         for m in range(a, b):
             sy.dma_start(T.wt[:, 512 * m:512 * m + 512], T.wa[128 * m:128 * m + 128, :]).then_inc(S.s_wa, 16)
 
     sy.dma_start(T.lt[me, 0:16, 0], T.tab[:, 0]).then_inc(S.s_lt, 16)
-    sy.dma_start(T.lt[me, 16:128, 0], T.tok[0, 0:112]).then_inc(S.s_lt, 16)
-    sy.dma_start(T.tr[0:1, 0:16], T.tab[:, 0]).then_inc(S.s_tr, 16)
     for q in range(4):
         sy.dma_start(T.tk[16 * q:16 * q + 16, :], T.tok[:]).then_inc(S.s_tk, 16)
+    sy.wait_ge(S.s_z, 2)
+    for q in range(2):
+        sy.dma_start(T.tr[32 * q:32 * q + 16, 0:1], T.tab[:, 0]).then_inc(S.s_tr, 16)
     sy.dma_start(T.xt[:], T.x[:]).then_inc(S.s_x, 16)
-    wa_load(0, 3)
-    sy.wait_ge(S.s_kv, 1)
-    sy.wait_ge(S.s_cf, 6)
-    for f, q in enumerate(full):
-        sy.dma_start(T.vl[16 * q:16 * q + 1, :], T.cf[0:1, 256 * f:256 * f + 256]).then_inc(S.s_vl, 16)
-    sy.wait_ge(S.s_go, 1)
-    wa_load(3, 6)
-    sy.wait_ge(S.s_li, 7)
     sy.wait_ge(S.s_lt, 32)
-    sy.dma_start(T.lr[0:1, 0:16], T.lt[:, 2 * me:2 * me + 2, 0]).then_inc(S.s_lr, 16)
-    wa_load(6, 8)
+    wa_load(0, WA_EARLY)
+    sy.wait_ge(S.s_go, 1)
+    wa_load(WA_EARLY, WA_MID)
+    sy.wait_ge(S.s_li, 7)
+    for q in range(4):
+        sy.dma_start(T.lr[32 * q:32 * q + 16, 0:1], T.lt[:, 2 * me:2 * me + 2, 0]).then_inc(S.s_lr, 16)
+    wa_load(WA_MID, 8)
     sy.wait_ge(S.s_w8, 1)
     for q in range(8):
         sy.dma_start(T.dd[:, q, :], T.w8[16 * q:16 * q + 1, 0:512]).then_inc(S.s_dd, 16)
@@ -195,99 +252,104 @@ def rank_program(g, core, T, topo):
     sy.dma_start(T.y[:, 0:256], T.yt[:, 0:256]).then_inc(S.s_y0, 16)
     sy.wait_ge(S.s_y0, 16)
 
-    def own_adapter(k):
-        g.indirect_dma_start(T.go[:, 512 * k:512 * k + 512], None, T.wa[:],
-                             IndirectOffsetOnAxis(ap=T.oi[:, k:k + 1], axis=0), bounds_check=1023).then_inc(S.s_own, 16)
+    def rows_of_wa(out, index, sem):
+        g.indirect_dma_start(out, None, T.wa[:], IndirectOffsetOnAxis(ap=index, axis=0), bounds_check=1023).then_inc(sem, 16)
 
     g.iota(T.pi[:], [[1, 1]], 0, 1).then_inc(S.s_k, 1)
     g.iota(T.bi[:], [[16, 32]], 0, 1).then_inc(S.s_k, 1)
-    g.iota(T.vl[:], [[1, 256]], 0, 16, allow_small_or_imprecise_dtypes=True).then_inc(S.s_kv, 1)
-    g.wait_ge(S.s_tr, 16)
-    g.partition_broadcast(T.ot[:], T.tr[0:1, 0:16], 128).then_inc(S.s_pb1, 1)
+    g.iota(T.vl[:], [[1, 256]], GB - 256 * len(full), 16, allow_small_or_imprecise_dtypes=True).then_inc(S.s_kv, 1)
     g.wait_ge(S.s_lt, 32)
     one = topo.engines(core, cores[order[0]])[:1]
     g.remote_dma_fused([RemoteDMATransfer(dst_ids=[dst(topo, cores[r], core) for r in order], dma_engine_mask=mask_of(one),
                                           remote_sem=S.s_li, srcs=[T.lt[me]], dsts=[T.lt[me] for r in order])],
                        local_sem=S.s_ls)
     g.sem_inc(S.s_go, 1)
-    g.wait_ge(S.s_oi, 1)
-    own_adapter(0)
-    g.wait_ge(S.s_lr, 16)
-    g.partition_broadcast(T.lb[:], T.lr[0:1, 0:16], 128).then_inc(S.s_pb2, 1)
-    own_adapter(1)
 
-    def move(pos, what, half):
-        a = (codes(T.qc[:, 256 * pos:256 * pos + 256]), T.qp[:, 256 * pos:256 * pos + 256])[what]
-        if pos in HOPS:
-            to = far
-            eng = on_chip(topo, core, to, cores[order[0]])
-            at = 256 * HOPS[pos]
-            b = (codes(T.hc[:, at:at + 256]), T.hp[:, at:at + 256])[what]
-            sem = S["h_%s%d" % ("cp"[what], pos)]
+    def move(piece):
+        pos, what, part = piece[:3]
+        if hops(piece):
+            to = hands[HOPS[pos]]
+            a, b = sides((T.qc, T.qp), (T.hc, T.hp), pos, sorted(HOPS).index(pos), what, part)
+            sem = S["h%d" % [x for x in pieces() if hops(x)].index(piece)]
         else:
             to = cores[order[pos]]
-            eng = topo.engines(core, to)
-            b = (codes(T.ic[:, 256 * me:256 * me + 256]), T.ip[:, 256 * me:256 * me + 256])[what]
+            a, b = sides((T.qc, T.qp), (T.ic, T.ip), pos, me, what, part)
             sem = S["ar%d" % me]
-        if half is not None:
-            w = len(eng) // 2
-            eng = eng[half * w:half * w + w]
+        eng = engines_of(piece, core, to, cores[order[pos]], topo)
         return RemoteDMATransfer(dst_ids=[dst(topo, to, core)], dma_engine_mask=mask_of(eng), remote_sem=sem, src=a, dst=b), len(eng)
 
     sent = 0
-    for call in CALLS:
+    for call in G_PLAN:
+        if call[0] == "i":
+            i, k = call[1:]
+            a = 2 * order[i] + k
+            g.wait_ge(S.s_ri, 1)
+            rows_of_wa(T.ga[:, 1024 * i + 512 * k:1024 * i + 512 * k + 512], T.ri[:, a:a + 1], S["gi%d" % i])
+            continue
+        if call[0] == "own":
+            k = call[1]
+            g.wait_ge(S.s_oi, 1)
+            rows_of_wa(T.go[:, 512 * k:512 * k + 512], T.oi[:, k:k + 1], S.s_own)
+            continue
         ts = []
-        for i, what, half in call:
-            g.wait_ge(S["vq%d" % i], 1)
-            t, n = move(i, what, half)
+        for piece in call:
+            g.wait_ge(S["vp%d" % piece[0] if piece[0] in EARLY and piece[2] == 0 else "vq%d" % piece[0]], 1)
+            t, n = move(piece)
             ts.append(t)
             sent += n
         g.remote_dma_fused(ts, local_sem=S.s_sent)
     g.wait_ge(S.s_ls, 1)
     g.wait_ge(S.s_sent, sent)
 
+    def xgather(k, t):
+        r, n = runs[k][0], len(runs[k])
+        at = 1024 * gathered.index(r)
+        return T.hx[:, at + t:at + 1024 * n:4], T.xt[:, t:2048].indirect(T.xo[:, 16 * r:16 * (r + n)])
+
+    def evac(n, k):
+        b = 2 * (n % 4) + k
+        if src[n] in full:
+            at, w = 1024 * full.index(src[n]) + 512 * k, 512
+        else:
+            at, w = GB + 128 * (2 * gathered.index(src[n]) + k), 128
+        return T.res[:, at:at + w], T.pm[:, 512 * b:512 * b + w]
+
+    def by_engines(i):
+        return [k for k in range(2) if ("i", i, k) not in G_PLAN]
+
+    def shared(q, copy, step):
+        if step[0] == "x":
+            copy(*xgather(step[1], step[2])).then_inc(S["gx%d" % step[1]], 1)
+        elif step[0] == "a":
+            i, lo, hi = step[1:]
+            q.wait_ge(S.s_wa, 128)
+            q.wait_ge(S["ao%d" % i], len(by_engines(i)))
+            copy(T.ga[:, 1024 * i + lo:1024 * i + hi],
+                 T.wt[:].indirect(T.ao[:, 64 * i + lo // 16:64 * i + hi // 16])).then_inc(S[("gp%d" if first(step) else "ga%d") % i], 1)
+        else:
+            q.wait_ge(S["mm%d" % (2 * step[1] + step[2])], 1)
+            copy(*evac(step[1], step[2])).then_inc(S["ev%d" % (2 * step[1] + step[2])], 1)
+
+    s.dma_start(T.lt[me, 16:128, 0], T.tok[0, 0:112]).then_inc(S.s_lt, 16)
     for q in range(4, 8):
         s.dma_start(T.tk[16 * q:16 * q + 16, :], T.tok[:]).then_inc(S.s_tk, 16)
-    for q in range(8):
-        s.dma_start(T.tg[16 * q:16 * q + 16, :], T.tok[:, 16 * q:16 * q + 16]).then_inc(S.s_tg, 16)
+    s.wait_ge(S.s_z, 2)
+    for q in range(2, 4):
+        s.dma_start(T.tr[32 * q:32 * q + 16, 0:1], T.tab[:, 0]).then_inc(S.s_tr, 16)
+    for q, r in enumerate(full + gathered):
+        s.dma_start(T.tg[16 * q:16 * q + 16, :], T.tok[:, 16 * r:16 * r + 16]).then_inc(S.s_tg, 16)
 
-    def xgather(k, t):
-        r, n = runs[k]
-        return (T.hx[:, 1024 * r + t:1024 * (r + n):4], T.xt[:, t:2048].indirect(T.xo[:, 16 * r:16 * (r + n)]))
+    def scopy(o, i):
+        return s.activation(o, i, COPY)
 
     s.wait_ge(S.s_xo, 1)
     s.wait_ge(S.s_x, 16)
-    for k, t in S_PRE:
-        o, i = xgather(k, t)
-        s.activation(o, i, COPY).then_inc(S["sx%d" % k], 1)
-    s.wait_ge(S.s_wa, 128)
-    for i in range(7):
-        s.wait_ge(S["ao%d" % i], 2)
-        s.activation(T.ga[:, 1024 * i:1024 * i + SPLIT],
-                     T.wt[:].indirect(T.ao[:, 64 * i:64 * i + SPLIT // 16]), COPY).then_inc(S["sa%d" % i], 1)
-    for k, t in S_POST:
-        o, i = xgather(k, t)
-        s.activation(o, i, COPY).then_inc(S["sx%d" % k], 1)
-
-    src = [me, order[2], order[4], order[0], order[1], order[5], order[3], order[6]]
-
-    def evac(k, n):
-        b = 2 * (n % 4) + k
-        if src[n] in full:
-            at, w = FB + 1024 * full.index(src[n]) + 512 * k, 512
-        else:
-            at, w = 128 * (2 * src[n] + k), 128
-        return T.res[:, at:at + w], T.pm[:, 512 * b:512 * b + w]
-
-    for n in range(NR):
-        s.wait_ge(S["mm%d" % n], 2)
-        o, i = evac(1, n)
-        s.activation(o, i, COPY).then_inc(S["ev%d" % n], 1)
+    for step in S_PLAN:
+        shared(s, scopy, step)
     s.wait_ge(S.s_po, 1)
-    s.wait_ge(S.s_ho, 3)
-    for n in range(NR):
-        s.wait_ge(S["ev%d" % n], 2)
-    s.activation(T.yt[:, 256:512], T.res[:].indirect(T.po[:, 16:32]), COPY).then_inc(S.s_ys, 1)
+    for n in range(2 * NR):
+        s.wait_ge(S["ev%d" % n], 1)
+    scopy(T.yt[:, 256:512], T.res[:].indirect(T.po[:, 16:32])).then_inc(S.s_ys, 1)
     s.wait_ge(S.s_ys, 1)
     s.dma_start(T.y[:, 256:512], T.yt[:, 256:512]).then_inc(S.s_y1, 16)
     s.wait_ge(S.s_y1, 16)
@@ -295,23 +357,24 @@ def rank_program(g, core, T, topo):
     for n in range(NR):
         r = src[n]
         if r in full:
-            pe.wait_ge(S.s_fq, 1)
+            pe.wait_ge(S.s_fq, 2)
         else:
             pe.wait_ge(S["xq%d" % run_of(r)], 1)
         if r == me:
             pe.wait_ge(S.s_oq, 1)
         else:
             pe.wait_ge(S["ar%d" % r], arrivals(r, me, cores, topo))
-        if n >= 4:
-            pe.wait_ge(S["ev%d" % (n - 4)], 2)
         for k in range(2):
+            if n >= 4:
+                pe.wait_ge(S["ev%d" % (2 * (n - 4) + k)], 1)
             c = 128 * (2 * r + k)
             b = 2 * (n % 4) + k
             if r in full:
                 o, xc, xp = T.pm[:, 512 * b:512 * b + 512], T.fc[:, 0:512], T.fp[:, 0:512]
             else:
-                o, xc, xp = T.pm[:, 512 * b:512 * b + 128], T.xc[:, c:c + 128], T.xp[:, c:c + 128]
-            pe.matmul_mx(o, T.ic[:, c:c + 128], T.ip[:, c:c + 128], xc, xp, True, True).then_inc(S["mm%d" % n], 1)
+                at = 128 * (2 * gathered.index(r) + k)
+                o, xc, xp = T.pm[:, 512 * b:512 * b + 128], T.xc[:, at:at + 128], T.xp[:, at:at + 128]
+            pe.matmul_mx(o, T.ic[:, c:c + 128], T.ip[:, c:c + 128], xc, xp, True, True).then_inc(S["mm%d" % (2 * n + k)], 1)
 
     cnt = [0]
 
@@ -322,114 +385,114 @@ def rank_program(g, core, T, topo):
     def done():
         v.wait_ge(S.vv, cnt[0])
 
+    def spread(z, col, out, factor):
+        dep(v.tensor_scalar(z[:], col[:, 0:4].indirect(T.z0[:, 0:2]), 0.0, factor, A.max, A.mult))
+        done()
+        dep(v.transpose(out[:], z[:]))
+        done()
+
+    v.memset(T.tr[:], 0).then_inc(S.s_z, 1)
+    v.memset(T.lr[:], 0).then_inc(S.s_z, 1)
+    dep(v.memset(T.z0[:], 0))
     dep(v.memset(T.w8[:, 0:512], 0.0))
-    for f in range(6):
-        v.memset(T.cf[:, 128 * f:128 * f + 128], float(FB + 512 * f)).then_inc(S.s_cf, 1)
     v.wait_ge(S.s_k, 2)
     dep(v.tensor_scalar(T.p112[:], T.pi[:], 112, None, A.bitwise_and))
     dep(v.tensor_copy(T.pf[:], T.pi[:]))
+    dep(v.tensor_scalar(T.c0[:], T.pi[:], 64.0, None, A.mult))
+    dep(v.tensor_scalar(T.c1[:], T.pi[:], 64.0, 512.0, A.mult, A.add))
     done()
     dep(v.tensor_copy(T.kf[:], T.p112[:]))
     done()
     dep(v.tensor_scalar(T.bo[:], T.bi[:], T.kf[:], None, A.subtract))
     done()
-    dep(v.tensor_scalar(T.j33[:], T.bo[:, 0:16], 33.0, None, A.add))
+    dep(v.tensor_scalar(T.jk[:], T.bo[:, 0:16], 512.0, None, A.add))
+    v.wait_ge(S.s_kv, 1)
+    top = 16 * len(full)
+    for k, c in enumerate((T.c0, T.c1)):
+        part = T.vl[0:top, 128 * k:128 * k + 128]
+        dep(v.tensor_scalar(part, part, 0.0, c[0:top, :], A.mult, A.add))
     v.wait_ge(S.s_tk, 128)
     v.tensor_scalar(T.xo[:], T.tk[:], 0.0, 4.0, A.max, A.mult).then_inc(S.s_xo, 1)
-    v.wait_ge(S.s_pb1, 1)
-    dep(v.tensor_scalar(T.oa[:], T.ot[:, 2 * me:2 * me + 2], 0.0, 128.0, A.max, A.mult))
+    v.wait_ge(S.s_tr, 64)
     done()
-    v.tensor_scalar(T.oi[:], T.oa[:], T.pf[:], None, A.add).then_inc(S.s_oi, 1)
-    for r in full:
-        v.memset(T.res[:, 256 * r:256 * r + 256], 0.0).then_inc(S.s_ho, 1)
-
+    spread(T.zo, T.tr, T.mo, 128.0)
+    v.tensor_scalar(T.oi[:], T.mo[:, 2 * me:2 * me + 2], T.pf[:], None, A.add).then_inc(S.s_oi, 1)
     v.wait_ge(S.s_xo, 1)
     v.wait_ge(S.s_x, 16)
 
-    def vx(lst):
-        for k, t in lst:
-            o, i = xgather(k, t)
-            v.tensor_copy(o, i).then_inc(S["vx%d" % k], 1)
-
     def xquant(k):
-        nv, ns = sum(1 for a in V_PRE + V_POST if a[0] == k), sum(1 for a in S_PRE + S_POST if a[0] == k)
-        if nv:
-            v.wait_ge(S["vx%d" % k], nv)
-        if ns:
-            v.wait_ge(S["sx%d" % k], ns)
-        r, n = runs[k]
-        v.quantize_mx(T.xc[:, 256 * r:256 * (r + n)], T.xp[:, 256 * r:256 * (r + n)],
-                      T.hx[:, 1024 * r:1024 * (r + n)]).then_inc(S["xq%d" % k], 1)
+        v.wait_ge(S["gx%d" % k], 4)
+        at, n = 256 * gathered.index(runs[k][0]), 256 * len(runs[k])
+        v.quantize_mx(T.xc[:, at:at + n], T.xp[:, at:at + n], T.hx[:, 4 * at:4 * (at + n)]).then_inc(S["xq%d" % k], 1)
 
-    vx(V_PRE)
-    v.quantize_mx(T.fc[:, 0:512], T.fp[:, 0:512], T.xt[:, 0:2048]).then_inc(S.s_fq, 1)
-    v.wait_ge(S.s_tg, 128)
-    dep(v.tensor_scalar(T.pb[:], T.tg[:], 4, None, A.arith_shift_right))
-    dep(v.tensor_scalar(T.pc[:], T.tg[:], 32.0, None, A.mult))
-    dep(v.tensor_scalar(T.pn[:], T.tg[:], 0.0, None, A.is_lt))
-    done()
-    dep(v.tensor_scalar(T.pd[:], T.pb[:], -511.0, None, A.mult))
-    dep(v.tensor_tensor(T.pj[:], T.pn[:], T.j33[:], A.mult))
-    done()
-    dep(v.tensor_tensor(T.pe[:], T.pc[:], T.pd[:], A.add))
-    done()
-    dep(v.tensor_tensor(T.ps[:], T.pe[:], T.pj[:], A.add))
-    done()
-    dep(v.tensor_copy(T.wo[:], T.ps[:]))
-    done()
-    v.wait_ge(S.s_kv, 1)
-    v.wait_ge(S.s_vl, 48)
-    v.tensor_copy(T.w8[:].indirect(T.wo[:]), T.vl[:]).then_inc(S.s_w8, 1)
-    xquant(0)
-
-    v.wait_ge(S.s_pb2, 1)
-    dep(v.tensor_scalar(T.mf[:], T.lb[:], 0.0, 512.0, A.max, A.mult))
-    done()
-
-    def offsets(i):
-        for k in range(2):
-            a = 2 * order[i] + k
-            c = 64 * i + 32 * k
-            v.tensor_scalar(T.ao[:, c:c + 32], T.bo[:], T.mf[:, a:a + 1], None, A.add).then_inc(S["ao%d" % i], 1)
-
-    offsets(0)
-    v.wait_ge(S.s_wa, 128)
-    for i in range(7):
-        if i < 6:
-            offsets(i + 1)
-        v.wait_ge(S["ao%d" % i], 2)
-        v.tensor_copy(T.ga[:, 1024 * i + SPLIT:1024 * i + 1024],
-                      T.wt[:].indirect(T.ao[:, 64 * i + SPLIT // 16:64 * i + 64])).then_inc(S["va%d" % i], 1)
-        v.wait_ge(S["va%d" % i], 1)
-        v.wait_ge(S["sa%d" % i], 1)
-        v.quantize_mx(T.qc[:, 256 * i:256 * i + 256], T.qp[:, 256 * i:256 * i + 256],
-                      T.ga[:, 1024 * i:1024 * i + 1024]).then_inc(S["vq%d" % i], 1)
-        if i == 3:
+    def vstep(step):
+        if step[0] == "xq":
+            xquant(step[1])
+        elif step[0] in ("x", "e", "a") and len(step) > 2:
+            shared(v, v.tensor_copy, step)
+        elif step == "list":
+            v.wait_ge(S.s_lr, 64)
+            spread(T.zl, T.lr, T.mf, 512.0)
+        elif step == "ri":
+            v.tensor_scalar(T.ri[:], T.mf[:, 0:16], 0.25, T.pf[:], A.mult, A.add).then_inc(S.s_ri, 1)
+        elif step[0] == "of":
+            i = step[1]
+            for k in by_engines(i):
+                a, c = 2 * order[i] + k, 64 * i + 32 * k
+                v.tensor_scalar(T.ao[:, c:c + 32], T.bo[:], T.mf[:, a:a + 1], None, A.add).then_inc(S["ao%d" % i], 1)
+        elif step[0] == "q":
+            i = step[1]
+            v.wait_ge(S["ga%d" % i], sum(1 for a in V_PLAN + S_PLAN if a[0] == "a" and a[1] == i and not first(a)))
+            if len(by_engines(i)) < 2:
+                v.wait_ge(S["gi%d" % i], 32 - 16 * len(by_engines(i)))
+            lo, hi = 256 * i + (128 if i in EARLY else 0), 256 * i + 256
+            v.quantize_mx(T.qc[:, lo:hi], T.qp[:, lo:hi], T.ga[:, 4 * lo:4 * hi]).then_inc(S["vq%d" % i], 1)
+        elif step[0] == "q0":
+            i = step[1]
+            v.wait_ge(S["gp%d" % i], sum(1 for a in V_PLAN + S_PLAN if a[0] == "a" and a[1] == i and first(a)))
+            lo, hi = 256 * i, 256 * i + 128
+            v.quantize_mx(T.qc[:, lo:hi], T.qp[:, lo:hi], T.ga[:, 4 * lo:4 * hi]).then_inc(S["vp%d" % i], 1)
+        elif step[0] == "fq":
+            at = 256 * step[1]
+            v.quantize_mx(T.fc[:, at:at + 256], T.fp[:, at:at + 256], T.xt[:, 4 * at:4 * at + 1024]).then_inc(S.s_fq, 1)
+        elif step == "oq":
             v.wait_ge(S.s_own, 32)
             v.quantize_mx(T.ic[:, 256 * me:256 * me + 256], T.ip[:, 256 * me:256 * me + 256], T.go[:]).then_inc(S.s_oq, 1)
-    vx(V_POST)
-    v.wait_ge(S.s_e8, 128)
-    dep(v.tensor_tensor(T.e4[:], T.e8[:, 0:128], T.e8[:, 128:256], A.add))
-    done()
-    dep(v.tensor_tensor(T.e2[:], T.e4[:, 0:64], T.e4[:, 64:128], A.add))
-    done()
-    dep(v.tensor_tensor(T.e1[:], T.e2[:, 0:32], T.e2[:, 32:64], A.add))
-    done()
-    dep(v.tensor_scalar(T.em[:], T.e1[:], float(FB), None, A.is_ge))
-    done()
-    dep(v.tensor_tensor(T.ei[:], T.em[:], T.bo[:], A.mult))
-    done()
-    dep(v.tensor_tensor(T.es[:], T.e1[:], T.ei[:], A.add))
-    done()
-    v.tensor_copy(T.po[:], T.es[:]).then_inc(S.s_po, 1)
-    xquant(1)
-    xquant(2)
-    for n in range(NR):
-        v.wait_ge(S["mm%d" % n], 2)
-        o, i = evac(0, n)
-        v.tensor_copy(o, i).then_inc(S["ev%d" % n], 1)
+        elif step == "o1":
+            v.wait_ge(S.s_tg, 128)
+            dep(v.tensor_scalar(T.pa[:], T.tg[:], 15, None, A.bitwise_and))
+            dep(v.tensor_scalar(T.pb[:], T.tg[:], 32767, 4, A.bitwise_and, A.arith_shift_right))
+        else:
+            done()
+            if step == "o2":
+                dep(v.tensor_scalar(T.pc[:], T.pa[:], 32.0, None, A.mult))
+            elif step == "o3":
+                dep(v.tensor_tensor(T.pd[:], T.pc[:], T.pb[:], A.add))
+            elif step == "o4":
+                dep(v.tensor_tensor(T.ps[:], T.pd[:], T.jk[:], A.min))
+            elif step == "o5":
+                dep(v.tensor_copy(T.wo[:], T.ps[:]))
+            elif step == "scatter":
+                v.tensor_copy(T.w8[:].indirect(T.wo[:]), T.vl[:]).then_inc(S.s_w8, 1)
+            elif step == "e4":
+                v.wait_ge(S.s_e8, 128)
+                dep(v.tensor_tensor(T.e4[:], T.e8[:, 0:128], T.e8[:, 128:256], A.add))
+            elif step == "e2":
+                dep(v.tensor_tensor(T.e2[:], T.e4[:, 0:64], T.e4[:, 64:128], A.add))
+            elif step == "e1":
+                dep(v.tensor_tensor(T.e1[:], T.e2[:, 0:32], T.e2[:, 32:64], A.add))
+            elif step == "em":
+                dep(v.tensor_scalar(T.em[:], T.e1[:], float(GB), None, A.is_lt))
+            elif step == "ei":
+                dep(v.tensor_tensor(T.ei[:], T.em[:], T.bo[:], A.mult))
+            elif step == "es":
+                dep(v.tensor_tensor(T.es[:], T.e1[:], T.ei[:], A.add))
+            elif step == "po":
+                v.tensor_copy(T.po[:], T.es[:]).then_inc(S.s_po, 1)
+
+    for step in V_PLAN:
+        vstep(step)
     v.wait_ge(S.s_po, 1)
-    v.wait_ge(S.s_ho, 3)
-    for n in range(NR):
-        v.wait_ge(S["ev%d" % n], 2)
+    for n in range(2 * NR):
+        v.wait_ge(S["ev%d" % n], 1)
     v.tensor_copy(T.yt[:, 0:256], T.res[:].indirect(T.po[:, 0:16])).then_inc(S.s_yv, 1)

from concourse.bass import DstId, RemoteDMATransfer, IndirectOffsetOnAxis
from concourse.mybir import dt, AluOpType, ActivationFunctionType

NR = 8
A = AluOpType
COPY = ActivationFunctionType.Copy
F8 = "float8_e4m3fn_x4"
GB = 3072

SCRATCH = {
    "xt": ("sbuf", [128, 2048], "bfloat16"),
    "wt": ("sbuf", [128, 4096], "bfloat16"),
    "lt": ("dram", [NR, 128, 1], "int32"),
    "tr": ("sbuf", [128, 4], "int32"),
    "lr": ("sbuf", [128, 4], "int32"),
    "zo": ("sbuf", [128, 32], "float32"),
    "mo": ("sbuf", [128, 32], "float32"),
    "zl": ("sbuf", [128, 32], "float32"),
    "mf": ("sbuf", [128, 32], "float32"),
    "oi": ("sbuf", [128, 2], "int32"),
    "ri": ("sbuf", [128, 16], "int32"),
    "tk": ("sbuf", [128, 128], "int32"),
    "xo": ("sbuf", [128, 128], "uint16"),
    "ao": ("sbuf", [128, 448], "uint16"),
    "z0": ("sbuf", [128, 2], "uint16"),
    "pi": ("sbuf", [128, 1], "int32"),
    "p112": ("sbuf", [128, 1], "int32"),
    "pf": ("sbuf", [128, 1], "float32"),
    "kf": ("sbuf", [128, 1], "float32"),
    "c0": ("sbuf", [128, 1], "float32"),
    "c1": ("sbuf", [128, 1], "float32"),
    "bi": ("sbuf", [128, 32], "int32"),
    "bo": ("sbuf", [128, 32], "int32"),
    "jk": ("sbuf", [128, 16], "int32"),
    "vl": ("sbuf", [128, 256], "float32"),
    "tg": ("sbuf", [128, 16], "int32"),
    "pa": ("sbuf", [128, 16], "int32"),
    "pb": ("sbuf", [128, 16], "int32"),
    "pc": ("sbuf", [128, 16], "int32"),
    "pd": ("sbuf", [128, 16], "int32"),
    "ps": ("sbuf", [128, 16], "int32"),
    "wo": ("sbuf", [128, 16], "uint16"),
    "w8": ("sbuf", [128, 768], "float32"),
    "dd": ("dram", [16, 8, 32], "float32"),
    "e8": ("sbuf", [128, 256], "float32"),
    "e4": ("sbuf", [128, 128], "float32"),
    "e2": ("sbuf", [128, 64], "float32"),
    "e1": ("sbuf", [128, 32], "float32"),
    "em": ("sbuf", [128, 32], "float32"),
    "ei": ("sbuf", [128, 32], "float32"),
    "es": ("sbuf", [128, 32], "float32"),
    "po": ("sbuf", [128, 32], "uint16"),
    "ga": ("sbuf", [128, 7 * 1024], "bfloat16"),
    "go": ("sbuf", [128, 1024], "bfloat16"),
    "qc": ("sbuf", [128, 7 * 256], F8),
    "qp": ("sbuf", [128, 7 * 256], "uint8"),
    "ic": ("sbuf", [128, 2048], F8),
    "ip": ("sbuf", [128, 2048], "uint8"),
    "hc": ("sbuf", [128, 1280], F8),
    "hp": ("sbuf", [128, 1280], "uint8"),
    "hx": ("sbuf", [128, 5120], "bfloat16"),
    "xc": ("sbuf", [128, 1280], F8),
    "xp": ("sbuf", [128, 1280], "uint8"),
    "fc": ("sbuf", [128, 512], F8),
    "fp": ("sbuf", [128, 512], "uint8"),
    "pm": ("psum", [128, 4096], "float32"),
    "res": ("sbuf", [128, GB + 1280], "float32"),
    "yt": ("sbuf", [128, 512], "float32"),
}

SEMAPHORES = (["s_lt", "s_tr", "s_x", "s_wa", "s_tk", "s_tg", "s_dd", "s_e8", "s_li", "s_lr", "s_y0", "s_y1", "s_own", "s_k",
               "s_z", "s_oi", "s_ri", "s_sent", "s_ls", "s_go", "vv", "s_xo", "s_w8", "s_po", "s_oq", "s_yv", "s_ys",
               "s_kv", "s_fq"] + ["h%d" % i for i in range(12)]
              + ["ar%d" % i for i in range(NR)] + ["mm%d" % i for i in range(2 * NR)] + ["ev%d" % i for i in range(2 * NR)]
              + ["ao%d" % i for i in range(7)] + ["ga%d" % i for i in range(7)]
              + ["vq%d" % i for i in range(7)] + ["gi%d" % i for i in range(7)]
              + ["vp%d" % i for i in range(7)] + ["gp%d" % i for i in range(7)]
              + ["gx%d" % i for i in range(3)] + ["xq%d" % i for i in range(3)])

ORDER = [("x", 2), ("x", 0), ("s", 1), ("s", 2), ("x", 1), ("s", 0), ("m", 0)]
HOPS = {0: 0, 1: 0, 3: 0}
HALF = {0: 0}
EARLY = [0]
FULL = [2, 4]
RUNS = [[0, 3], [1, 5], [6]]
SRC = [-1, 2, 4, 0, 1, 5, 3, 6]
WA_EARLY = 1
WA_MID = 7


def cod(*pos):
    return [(i, 0, None, None) for i in pos]


def pla(*pos):
    return [(i, 1, None, None) for i in pos]


G_PLAN = [("own", 0), ("own", 1), [(0, 0, 0, None)], [(0, 0, 1, None)], pla(0),
          cod(1, 2), pla(1, 2), cod(3), cod(4), pla(3, 4), cod(5), pla(5), cod(6), pla(6)]
SHARE = {1: 672, 2: 672, 3: 672, 4: 672, 5: 640, 6: 640}
S_PLAN = ([("x", 0, 0), ("x", 0, 1), ("x", 0, 2), ("x", 1, 0), ("x", 1, 1), ("a", 0, 0, 224), ("a", 0, 512, 800)]
          + [("a", i, 0, SHARE[i]) for i in range(1, 7)]
          + [("x", 1, 2), ("x", 2, 0), ("x", 2, 1), ("x", 2, 2), ("x", 2, 3)] + [("e", n, 1) for n in range(8)])
V_PLAN = ([("x", 0, 3), "o1", ("fq", 0), "o2", ("fq", 1), "o3", "o4", "o5", "scatter", ("xq", 0), "list"]
          + [("of", 0), ("of", 1), ("a", 0, 224, 512), ("q0", 0), ("a", 0, 800, 1024), ("of", 2), ("q", 0)]
          + [x for i in range(1, 5) for x in (("a", i, SHARE[i], 1024), ("of", i + 2), ("q", i))]
          + [x for i in range(5, 7) for x in (("a", i, SHARE[i], 1024), ("q", i))]
          + ["oq", ("x", 1, 3), "e4", ("xq", 1), "e2", ("e", 0, 0), "e1", ("e", 1, 0), "em", ("xq", 2), "ei", ("e", 2, 0), "es",
             ("e", 3, 0), "po"] + [("e", n, 0) for n in range(4, 8)])


def mask_of(engines):
    return sum(1 << e for e in engines)


def roads(me, cores, topo):
    c = cores[me]
    others = sorted([r for r in range(NR) if r != me], key=lambda r: r ^ me)
    mate = [r for r in others if topo.mates(c, cores[r])]
    same = [r for r in others if topo.same_plane(c, cores[r])]
    cross = [[q for q in others if topo.mates(cores[r], cores[q])][0] for r in same]
    free = [h for h in topo.cores_of(c) if h != c and all(topo.may_write(h, cores[r]) for r in others)]
    hands = [h for h in free if topo.die(h) != topo.die(c)] + [h for h in free if topo.die(h) == topo.die(c)]
    return [{"s": same, "x": cross, "m": mate}[kind][k] for kind, k in ORDER], hands


def dst(topo, d, src):
    rid, pid = topo.addr(d, src)
    return DstId(rid=rid, pnc=pid)


def codes(v):
    return v.bitcast(dt.uint8)


def hops(piece):
    return piece[0] in HOPS and HALF.get(piece[0], piece[2]) == piece[2]


def first(step):
    return step[1] in EARLY and step[3] <= 512


def pieces():
    return [x for call in G_PLAN if call[0] not in ("i", "own") for x in call]


def sides(a, b, i, j, what, part):
    lo, w = (0, 256) if part is None else (128 * part, 128)
    s, d = a[what][:, 256 * i + lo:256 * i + lo + w], b[what][:, 256 * j + lo:256 * j + lo + w]
    return (s, d) if what else (codes(s), codes(d))


def engines_of(piece, src, to, away, topo):
    eng = topo.engines(src, to)
    if piece[3] == "out":
        eng = topo.engines(src, away)
    elif hops(piece) and piece[3] != "all":
        eng = [e for e in eng if e not in topo.engines(src, away)]
    if piece[3] in (0, 1):
        w = len(eng) // 2
        eng = eng[piece[3] * w:piece[3] * w + w]
    return eng


def onward(piece, hand, to, topo):
    call = [c for c in G_PLAN if piece in c][0]
    both = [x for x in call if hops(x) and HOPS[x[0]] == HOPS[piece[0]]]
    eng = topo.engines(hand, to)
    w = len(eng) // len(both)
    return eng[w * both.index(piece):w * both.index(piece) + w]


def helper_program(g, core, T, topo, me):
    cores = list(T.cores)
    order, hands = roads(me, cores, topo)
    sent = 0
    hopping = [x for x in pieces() if hops(x)]
    for call in G_PLAN:
        ts = []
        for piece in call:
            if piece not in hopping or hands[HOPS[piece[0]]] != core:
                continue
            pos, what, part = piece[:3]
            r = order[pos]
            eng = onward(piece, core, cores[r], topo)
            g.wait_ge(T.sem["h%d" % hopping.index(piece)], len(engines_of(piece, cores[me], core, cores[r], topo)))
            s, d = sides((T.hc, T.hp), (T.ic, T.ip), sorted(HOPS).index(pos), me, what, part)
            ts.append(RemoteDMATransfer(dst_ids=[dst(topo, cores[r], core)], dma_engine_mask=mask_of(eng),
                                        remote_sem=T.sem["ar%d" % me], src=s, dst=d))
            sent += len(eng)
        if ts:
            g.remote_dma_fused(ts, local_sem=T.sem.s_sent)
    if sent:
        g.wait_ge(T.sem.s_sent, sent)


def arrivals(r, me, cores, topo):
    order, hands = roads(r, cores, topo)
    pos = order.index(me)
    return sum(len(onward(x, hands[HOPS[pos]], cores[me], topo) if hops(x) else engines_of(x, cores[r], cores[me], cores[me], topo))
               for x in pieces() if x[0] == pos)


def rank_program(g, core, T, topo):
    rank = T.rank_of(core)
    cores = list(T.cores)
    if rank is None:
        for r in range(NR):
            if core in topo.cores_of(cores[r]):
                helper_program(g, core, T, topo, r)
        return
    me = rank
    order, hands = roads(me, cores, topo)
    S = T.sem
    v, s, pe, sy = g.vector, g.scalar, g.tensor, g.sync
    full = [me] + [order[i] for i in FULL]
    runs = [sorted(order[i] for i in run) for run in RUNS]
    gathered = [r for run in runs for r in run]
    src = [me if i < 0 else order[i] for i in SRC]

    def run_of(r):
        return [k for k in range(3) if r in runs[k]][0]

    def wa_load(a, b):
        for m in range(a, b):
            sy.dma_start(T.wt[:, 512 * m:512 * m + 512], T.wa[128 * m:128 * m + 128, :]).then_inc(S.s_wa, 16)

    sy.dma_start(T.lt[me, 0:16, 0], T.tab[:, 0]).then_inc(S.s_lt, 16)
    for q in range(4):
        sy.dma_start(T.tk[16 * q:16 * q + 16, :], T.tok[:]).then_inc(S.s_tk, 16)
    sy.wait_ge(S.s_z, 2)
    for q in range(2):
        sy.dma_start(T.tr[32 * q:32 * q + 16, 0:1], T.tab[:, 0]).then_inc(S.s_tr, 16)
    sy.dma_start(T.xt[:], T.x[:]).then_inc(S.s_x, 16)
    sy.wait_ge(S.s_lt, 32)
    wa_load(0, WA_EARLY)
    sy.wait_ge(S.s_go, 1)
    wa_load(WA_EARLY, WA_MID)
    sy.wait_ge(S.s_li, 7)
    for q in range(4):
        sy.dma_start(T.lr[32 * q:32 * q + 16, 0:1], T.lt[:, 2 * me:2 * me + 2, 0]).then_inc(S.s_lr, 16)
    wa_load(WA_MID, 8)
    sy.wait_ge(S.s_w8, 1)
    for q in range(8):
        sy.dma_start(T.dd[:, q, :], T.w8[16 * q:16 * q + 1, 0:512]).then_inc(S.s_dd, 16)
    sy.wait_ge(S.s_dd, 128)
    for q in range(8):
        sy.dma_start(T.e8[16 * q:16 * q + 16, 0:256], T.dd[:]).then_inc(S.s_e8, 16)
    sy.wait_ge(S.s_yv, 1)
    sy.dma_start(T.y[:, 0:256], T.yt[:, 0:256]).then_inc(S.s_y0, 16)
    sy.wait_ge(S.s_y0, 16)

    def rows_of_wa(out, index, sem):
        g.indirect_dma_start(out, None, T.wa[:], IndirectOffsetOnAxis(ap=index, axis=0), bounds_check=1023).then_inc(sem, 16)

    g.iota(T.pi[:], [[1, 1]], 0, 1).then_inc(S.s_k, 1)
    g.iota(T.bi[:], [[16, 32]], 0, 1).then_inc(S.s_k, 1)
    g.iota(T.vl[:], [[1, 256]], GB - 256 * len(full), 16, allow_small_or_imprecise_dtypes=True).then_inc(S.s_kv, 1)
    g.wait_ge(S.s_lt, 32)
    one = topo.engines(core, cores[order[0]])[:1]
    g.remote_dma_fused([RemoteDMATransfer(dst_ids=[dst(topo, cores[r], core) for r in order], dma_engine_mask=mask_of(one),
                                          remote_sem=S.s_li, srcs=[T.lt[me]], dsts=[T.lt[me] for r in order])],
                       local_sem=S.s_ls)
    g.sem_inc(S.s_go, 1)

    def move(piece):
        pos, what, part = piece[:3]
        if hops(piece):
            to = hands[HOPS[pos]]
            a, b = sides((T.qc, T.qp), (T.hc, T.hp), pos, sorted(HOPS).index(pos), what, part)
            sem = S["h%d" % [x for x in pieces() if hops(x)].index(piece)]
        else:
            to = cores[order[pos]]
            a, b = sides((T.qc, T.qp), (T.ic, T.ip), pos, me, what, part)
            sem = S["ar%d" % me]
        eng = engines_of(piece, core, to, cores[order[pos]], topo)
        return RemoteDMATransfer(dst_ids=[dst(topo, to, core)], dma_engine_mask=mask_of(eng), remote_sem=sem, src=a, dst=b), len(eng)

    sent = 0
    for call in G_PLAN:
        if call[0] == "i":
            i, k = call[1:]
            a = 2 * order[i] + k
            g.wait_ge(S.s_ri, 1)
            rows_of_wa(T.ga[:, 1024 * i + 512 * k:1024 * i + 512 * k + 512], T.ri[:, a:a + 1], S["gi%d" % i])
            continue
        if call[0] == "own":
            k = call[1]
            g.wait_ge(S.s_oi, 1)
            rows_of_wa(T.go[:, 512 * k:512 * k + 512], T.oi[:, k:k + 1], S.s_own)
            continue
        ts = []
        for piece in call:
            g.wait_ge(S["vp%d" % piece[0] if piece[0] in EARLY and piece[2] == 0 else "vq%d" % piece[0]], 1)
            t, n = move(piece)
            ts.append(t)
            sent += n
        g.remote_dma_fused(ts, local_sem=S.s_sent)
    g.wait_ge(S.s_ls, 1)
    g.wait_ge(S.s_sent, sent)

    def xgather(k, t):
        r, n = runs[k][0], len(runs[k])
        at = 1024 * gathered.index(r)
        return T.hx[:, at + t:at + 1024 * n:4], T.xt[:, t:2048].indirect(T.xo[:, 16 * r:16 * (r + n)])

    def evac(n, k):
        b = 2 * (n % 4) + k
        if src[n] in full:
            at, w = 1024 * full.index(src[n]) + 512 * k, 512
        else:
            at, w = GB + 128 * (2 * gathered.index(src[n]) + k), 128
        return T.res[:, at:at + w], T.pm[:, 512 * b:512 * b + w]

    def by_engines(i):
        return [k for k in range(2) if ("i", i, k) not in G_PLAN]

    def shared(q, copy, step):
        if step[0] == "x":
            copy(*xgather(step[1], step[2])).then_inc(S["gx%d" % step[1]], 1)
        elif step[0] == "a":
            i, lo, hi = step[1:]
            q.wait_ge(S.s_wa, 128)
            q.wait_ge(S["ao%d" % i], len(by_engines(i)))
            copy(T.ga[:, 1024 * i + lo:1024 * i + hi],
                 T.wt[:].indirect(T.ao[:, 64 * i + lo // 16:64 * i + hi // 16])).then_inc(S[("gp%d" if first(step) else "ga%d") % i], 1)
        else:
            q.wait_ge(S["mm%d" % (2 * step[1] + step[2])], 1)
            copy(*evac(step[1], step[2])).then_inc(S["ev%d" % (2 * step[1] + step[2])], 1)

    s.dma_start(T.lt[me, 16:128, 0], T.tok[0, 0:112]).then_inc(S.s_lt, 16)
    for q in range(4, 8):
        s.dma_start(T.tk[16 * q:16 * q + 16, :], T.tok[:]).then_inc(S.s_tk, 16)
    s.wait_ge(S.s_z, 2)
    for q in range(2, 4):
        s.dma_start(T.tr[32 * q:32 * q + 16, 0:1], T.tab[:, 0]).then_inc(S.s_tr, 16)
    for q, r in enumerate(full + gathered):
        s.dma_start(T.tg[16 * q:16 * q + 16, :], T.tok[:, 16 * r:16 * r + 16]).then_inc(S.s_tg, 16)

    def scopy(o, i):
        return s.activation(o, i, COPY)

    s.wait_ge(S.s_xo, 1)
    s.wait_ge(S.s_x, 16)
    for step in S_PLAN:
        shared(s, scopy, step)
    s.wait_ge(S.s_po, 1)
    for n in range(2 * NR):
        s.wait_ge(S["ev%d" % n], 1)
    scopy(T.yt[:, 256:512], T.res[:].indirect(T.po[:, 16:32])).then_inc(S.s_ys, 1)
    s.wait_ge(S.s_ys, 1)
    s.dma_start(T.y[:, 256:512], T.yt[:, 256:512]).then_inc(S.s_y1, 16)
    s.wait_ge(S.s_y1, 16)

    for n in range(NR):
        r = src[n]
        if r in full:
            pe.wait_ge(S.s_fq, 2)
        else:
            pe.wait_ge(S["xq%d" % run_of(r)], 1)
        if r == me:
            pe.wait_ge(S.s_oq, 1)
        else:
            pe.wait_ge(S["ar%d" % r], arrivals(r, me, cores, topo))
        for k in range(2):
            if n >= 4:
                pe.wait_ge(S["ev%d" % (2 * (n - 4) + k)], 1)
            c = 128 * (2 * r + k)
            b = 2 * (n % 4) + k
            if r in full:
                o, xc, xp = T.pm[:, 512 * b:512 * b + 512], T.fc[:, 0:512], T.fp[:, 0:512]
            else:
                at = 128 * (2 * gathered.index(r) + k)
                o, xc, xp = T.pm[:, 512 * b:512 * b + 128], T.xc[:, at:at + 128], T.xp[:, at:at + 128]
            pe.matmul_mx(o, T.ic[:, c:c + 128], T.ip[:, c:c + 128], xc, xp, True, True).then_inc(S["mm%d" % (2 * n + k)], 1)

    cnt = [0]

    def dep(inst):
        inst.then_inc(S.vv, 1)
        cnt[0] += 1

    def done():
        v.wait_ge(S.vv, cnt[0])

    def spread(z, col, out, factor):
        dep(v.tensor_scalar(z[:], col[:, 0:4].indirect(T.z0[:, 0:2]), 0.0, factor, A.max, A.mult))
        done()
        dep(v.transpose(out[:], z[:]))
        done()

    v.memset(T.tr[:], 0).then_inc(S.s_z, 1)
    v.memset(T.lr[:], 0).then_inc(S.s_z, 1)
    dep(v.memset(T.z0[:], 0))
    dep(v.memset(T.w8[:, 0:512], 0.0))
    v.wait_ge(S.s_k, 2)
    dep(v.tensor_scalar(T.p112[:], T.pi[:], 112, None, A.bitwise_and))
    dep(v.tensor_copy(T.pf[:], T.pi[:]))
    dep(v.tensor_scalar(T.c0[:], T.pi[:], 64.0, None, A.mult))
    dep(v.tensor_scalar(T.c1[:], T.pi[:], 64.0, 512.0, A.mult, A.add))
    done()
    dep(v.tensor_copy(T.kf[:], T.p112[:]))
    done()
    dep(v.tensor_scalar(T.bo[:], T.bi[:], T.kf[:], None, A.subtract))
    done()
    dep(v.tensor_scalar(T.jk[:], T.bo[:, 0:16], 512.0, None, A.add))
    v.wait_ge(S.s_kv, 1)
    top = 16 * len(full)
    for k, c in enumerate((T.c0, T.c1)):
        part = T.vl[0:top, 128 * k:128 * k + 128]
        dep(v.tensor_scalar(part, part, 0.0, c[0:top, :], A.mult, A.add))
    v.wait_ge(S.s_tk, 128)
    v.tensor_scalar(T.xo[:], T.tk[:], 0.0, 4.0, A.max, A.mult).then_inc(S.s_xo, 1)
    v.wait_ge(S.s_tr, 64)
    done()
    spread(T.zo, T.tr, T.mo, 128.0)
    v.tensor_scalar(T.oi[:], T.mo[:, 2 * me:2 * me + 2], T.pf[:], None, A.add).then_inc(S.s_oi, 1)
    v.wait_ge(S.s_xo, 1)
    v.wait_ge(S.s_x, 16)

    def xquant(k):
        v.wait_ge(S["gx%d" % k], 4)
        at, n = 256 * gathered.index(runs[k][0]), 256 * len(runs[k])
        v.quantize_mx(T.xc[:, at:at + n], T.xp[:, at:at + n], T.hx[:, 4 * at:4 * (at + n)]).then_inc(S["xq%d" % k], 1)

    def vstep(step):
        if step[0] == "xq":
            xquant(step[1])
        elif step[0] in ("x", "e", "a") and len(step) > 2:
            shared(v, v.tensor_copy, step)
        elif step == "list":
            v.wait_ge(S.s_lr, 64)
            spread(T.zl, T.lr, T.mf, 512.0)
        elif step == "ri":
            v.tensor_scalar(T.ri[:], T.mf[:, 0:16], 0.25, T.pf[:], A.mult, A.add).then_inc(S.s_ri, 1)
        elif step[0] == "of":
            i = step[1]
            for k in by_engines(i):
                a, c = 2 * order[i] + k, 64 * i + 32 * k
                v.tensor_scalar(T.ao[:, c:c + 32], T.bo[:], T.mf[:, a:a + 1], None, A.add).then_inc(S["ao%d" % i], 1)
        elif step[0] == "q":
            i = step[1]
            v.wait_ge(S["ga%d" % i], sum(1 for a in V_PLAN + S_PLAN if a[0] == "a" and a[1] == i and not first(a)))
            if len(by_engines(i)) < 2:
                v.wait_ge(S["gi%d" % i], 32 - 16 * len(by_engines(i)))
            lo, hi = 256 * i + (128 if i in EARLY else 0), 256 * i + 256
            v.quantize_mx(T.qc[:, lo:hi], T.qp[:, lo:hi], T.ga[:, 4 * lo:4 * hi]).then_inc(S["vq%d" % i], 1)
        elif step[0] == "q0":
            i = step[1]
            v.wait_ge(S["gp%d" % i], sum(1 for a in V_PLAN + S_PLAN if a[0] == "a" and a[1] == i and first(a)))
            lo, hi = 256 * i, 256 * i + 128
            v.quantize_mx(T.qc[:, lo:hi], T.qp[:, lo:hi], T.ga[:, 4 * lo:4 * hi]).then_inc(S["vp%d" % i], 1)
        elif step[0] == "fq":
            at = 256 * step[1]
            v.quantize_mx(T.fc[:, at:at + 256], T.fp[:, at:at + 256], T.xt[:, 4 * at:4 * at + 1024]).then_inc(S.s_fq, 1)
        elif step == "oq":
            v.wait_ge(S.s_own, 32)
            v.quantize_mx(T.ic[:, 256 * me:256 * me + 256], T.ip[:, 256 * me:256 * me + 256], T.go[:]).then_inc(S.s_oq, 1)
        elif step == "o1":
            v.wait_ge(S.s_tg, 128)
            dep(v.tensor_scalar(T.pa[:], T.tg[:], 15, None, A.bitwise_and))
            dep(v.tensor_scalar(T.pb[:], T.tg[:], 32767, 4, A.bitwise_and, A.arith_shift_right))
        else:
            done()
            if step == "o2":
                dep(v.tensor_scalar(T.pc[:], T.pa[:], 32.0, None, A.mult))
            elif step == "o3":
                dep(v.tensor_tensor(T.pd[:], T.pc[:], T.pb[:], A.add))
            elif step == "o4":
                dep(v.tensor_tensor(T.ps[:], T.pd[:], T.jk[:], A.min))
            elif step == "o5":
                dep(v.tensor_copy(T.wo[:], T.ps[:]))
            elif step == "scatter":
                v.tensor_copy(T.w8[:].indirect(T.wo[:]), T.vl[:]).then_inc(S.s_w8, 1)
            elif step == "e4":
                v.wait_ge(S.s_e8, 128)
                dep(v.tensor_tensor(T.e4[:], T.e8[:, 0:128], T.e8[:, 128:256], A.add))
            elif step == "e2":
                dep(v.tensor_tensor(T.e2[:], T.e4[:, 0:64], T.e4[:, 64:128], A.add))
            elif step == "e1":
                dep(v.tensor_tensor(T.e1[:], T.e2[:, 0:32], T.e2[:, 32:64], A.add))
            elif step == "em":
                dep(v.tensor_scalar(T.em[:], T.e1[:], float(GB), None, A.is_lt))
            elif step == "ei":
                dep(v.tensor_tensor(T.ei[:], T.em[:], T.bo[:], A.mult))
            elif step == "es":
                dep(v.tensor_tensor(T.es[:], T.e1[:], T.ei[:], A.add))
            elif step == "po":
                v.tensor_copy(T.po[:], T.es[:]).then_inc(S.s_po, 1)

    for step in V_PLAN:
        vstep(step)
    v.wait_ge(S.s_po, 1)
    for n in range(2 * NR):
        v.wait_ge(S["ev%d" % n], 1)
    v.tensor_copy(T.yt[:, 0:256], T.res[:].indirect(T.po[:, 0:16])).then_inc(S.s_yv, 1)
